import numpy as np
import ml_dtypes


def mxq(x, axis, fmt="e4m3"):
    dtype, down = {"e4m3": (ml_dtypes.float8_e4m3fn, 7), "e5m2": (ml_dtypes.float8_e5m2, 14)}[fmt]
    v = np.moveaxis(np.asarray(x, np.float32).astype(ml_dtypes.bfloat16).astype(np.float64), axis, -1)
    blocks = v.reshape(v.shape[:-1] + (-1, 32))
    amax = np.abs(blocks).max(-1, keepdims=True)
    byte = np.maximum(np.where(amax > 0, np.frexp(amax)[1] - 1 + 127, 0) - down, 1)
    scale = np.exp2(byte - 127.0)
    codes = (blocks / scale).astype(np.float32).astype(dtype).astype(np.float64)
    return np.moveaxis((codes * scale).reshape(v.shape), -1, axis)


WIDE = False


def mx_kscale(k):
    if not WIDE:
        return np.ones(k)
    levels = np.array([10, -10, 5, -5, 0])
    if k % 512:
        return np.exp2(np.random.permutation(np.resize(levels, k // 32))).repeat(32)
    a = np.empty((k // 512, 16))
    for p in range(k // 512):
        a[p, :8] = np.random.permutation(np.resize(levels, 8))
        for g in range(8):
            far = levels[np.abs(levels - a[p, g]) >= 10]
            a[p, g + 8] = far[np.random.randint(len(far))]
    return np.exp2(a.ravel()).repeat(32)


def f64(x):
    return np.asarray(x).astype(np.float64)


def striped(idx):
    return np.tile(idx.reshape(-1, 16).T, (8, 1)).astype(np.uint16)


def unstriped(offs):
    return offs[:16].T.reshape(-1).astype(np.int64)


def silu(v):
    return v / (1.0 + np.exp(-np.maximum(v, -700.0)))


K, T, S, N = 512, 1024, 512, 256


def setup_inputs():
    n = np.random.standard_normal
    s = mx_kscale(K)[:, None]
    return {
        "xT": (n((K, S)) * s).astype(np.float32),
        "w": (n((K, N)) / np.sqrt(K) / s).astype(np.float32),
        "b": (0.3 * n((N, 1))).astype(np.float32),
        "gate": np.tile(np.random.uniform(0.2, 1.0, S), (N, 1)).astype(np.float32),
        "offs": striped(np.random.permutation(T)[:S]),
    }


def reference(xT, w, b, gate, offs):
    idx = unstriped(offs)
    xq = mxq(f64(xT), 0, "e4m3")
    y = mxq(f64(w), 0, "e4m3").T @ xq
    y = silu(y + f64(b))
    out = np.zeros((N, T))
    out[:, idx] = f64(gate) * y
    return out

@@ -1,0 +1,114 @@
+from contextlib import ExitStack
+
+import concourse.mybir as mybir
+
+K, T, S, M = 512, 1024, 512, 256
+FLOPS = 2 * K * S * M
+
+F32 = mybir.dt.float32
+BF16 = mybir.dt.bfloat16
+U32 = mybir.dt.uint32
+U16 = mybir.dt.uint16
+U8 = mybir.dt.uint8
+FP8X4 = mybir.dt.float8_e4m3fn_x4
+SILU = mybir.ActivationFunctionType.Silu
+MULT = mybir.AluOpType.mult
+
+P = 128
+PACK = 4
+BLOCKS = M // P
+CHUNKS = ((0, 128), (128, 128), (256, 128), (384, 128))
+
+
+def tile_picked_place_lin_silu_sub_l_kernel(tc, xT, w, b, gate, offs, out):
+    nc = tc.nc
+    with ExitStack() as ctx:
+        keep = ctx.enter_context(tc.tile_pool(name="keep", bufs=1))
+        psum = ctx.enter_context(tc.psum_pool(name="psum", bufs=1))
+
+        offsets = keep.tile([P, S // 16], U16, name="offsets")
+        w_raw = keep.tile([P, PACK, M], F32, name="w_raw", align_bytes=64)
+        w_bf = keep.tile([P, M, PACK], BF16, name="w_bf", align_bytes=64)
+        w_codes = keep.tile([P, M], U32, name="w_codes", align_bytes=64)
+        w_scales = keep.tile([P, M], U8, name="w_scales", align_bytes=64)
+        x_codes = keep.tile([P, S], U32, name="x_codes", align_bytes=64)
+        x_scales = keep.tile([P, S], U8, name="x_scales", align_bytes=64)
+        x_raw = [keep.tile([P, PACK, n], F32, name=f"x_raw{c}", align_bytes=64) for c, (s0, n) in enumerate(CHUNKS)]
+        x_bf = [keep.tile([P, n, PACK], BF16, name=f"x_bf{c}", align_bytes=64) for c, (s0, n) in enumerate(CHUNKS)]
+        bias = [keep.tile([P, 1], F32, name=f"bias{m}") for m in range(BLOCKS)]
+        gates = [keep.tile([P, S], F32, name=f"gate{m}", align_bytes=64) for m in range(BLOCKS)]
+        window = [keep.tile([P, T], F32, name=f"window{m}", align_bytes=64) for m in range(BLOCKS)]
+        warm = keep.tile([P, 1], F32, name="warm")
+        warm_out = keep.tile([P, 1], F32, name="warm_out")
+
+        def load_x(c):
+            s0, n = CHUNKS[c]
+            nc.sync.dma_start(x_raw[c][:], xT[:, s0 : s0 + n].rearrange("(p j) n -> p j n", j=PACK))
+
+        nc.sync.dma_start(w_raw[:], w.rearrange("(p j) m -> p j m", j=PACK))
+        load_x(0)
+        nc.sync.dma_start(offsets[:], offs)
+        load_x(1)
+        nc.sync.dma_start(gates[0][:], gate[0:P, :])
+        nc.sync.dma_start(gates[1][:], gate[P : 2 * P, :])
+        load_x(2)
+        load_x(3)
+        for m in range(BLOCKS):
+            nc.scalar.dma_start(bias[m][:], b[m * P : (m + 1) * P, :])
+
+        nc.vector.memset(warm[:], 0.0)
+        nc.scalar.activation(warm_out[:], warm[:], SILU)
+        for m in range(BLOCKS):
+            nc.vector.memset(window[m][:], 0.0)
+
+        def interleave(copy, dst, src, lo, hi):
+            copy(dst[:, lo:hi, :], src[:, :, lo:hi].rearrange("p j n -> p n j"))
+
+        def quantize(dst, scales, src, lo, hi):
+            nc.vector.quantize_mx(
+                out=dst[:, lo:hi].bitcast(FP8X4),
+                scales=scales[:, lo:hi],
+                in_=src[:].rearrange("p n j -> p (n j)"),
+            )
+
+        interleave(nc.scalar.copy, w_bf, w_raw, 0, P)
+        interleave(nc.vector.tensor_copy, w_bf, w_raw, P, M)
+        quantize(w_codes, w_scales, w_bf, 0, M)
+        def prepare(c):
+            s0, n = CHUNKS[c]
+            interleave(nc.vector.tensor_copy if c < 2 else nc.scalar.copy, x_bf[c], x_raw[c], 0, n)
+            quantize(x_codes, x_scales, x_bf[c], s0, s0 + n)
+
+        prepare(0)
+        pending = []
+        for c, (s0, n) in enumerate(CHUNKS):
+            ys = []
+            for m in range(BLOCKS):
+                acc = psum.tile([P, n], F32, name=f"acc{c}_{m}")
+                nc.tensor.matmul_mx(
+                    out=acc[:],
+                    lhsT=w_codes[:, m * P : (m + 1) * P].bitcast(FP8X4),
+                    lhsT_scale=w_scales[:, m * P : (m + 1) * P],
+                    rhs=x_codes[:, s0 : s0 + n].bitcast(FP8X4),
+                    rhs_scale=x_scales[:, s0 : s0 + n],
+                    start=True,
+                    stop=True,
+                )
+                y = keep.tile([P, n], F32, name=f"y{c}_{m}", align_bytes=64)
+                nc.scalar.activation(y[:], acc[:], SILU, bias=bias[m][:])
+                ys.append(y)
+            if c + 1 < len(CHUNKS):
+                prepare(c + 1)
+            pending.append((s0, n, ys))
+            if c != len(CHUNKS) - 2:
+                for m in range(BLOCKS):
+                    for p0, pn, pys in pending:
+                        nc.vector.tensor_tensor(
+                            window[m][:].indirect(offsets[:, p0 // 16 : (p0 + pn) // 16]),
+                            pys[m][:],
+                            gates[m][:, p0 : p0 + pn],
+                            MULT,
+                        )
+                    if c == len(CHUNKS) - 1:
+                        nc.sync.dma_start(out[m * P : (m + 1) * P, :], window[m][:])
+                pending = []

@@ -17,7 +17,7 @@ MULT = mybir.AluOpType.mult
 P = 128
 PACK = 4
 BLOCKS = M // P
-CHUNKS = ((0, 128), (128, 128), (256, 128), (384, 128))
+X_CHUNKS = ((0, 128), (128, 128), (256, 128), (384, 128))
 
 
 def tile_picked_place_lin_silu_sub_l_kernel(tc, xT, w, b, gate, offs, out):
@@ -27,88 +27,112 @@ def tile_picked_place_lin_silu_sub_l_kernel(tc, xT, w, b, gate, offs, out):
         psum = ctx.enter_context(tc.psum_pool(name="psum", bufs=1))
 
         offsets = keep.tile([P, S // 16], U16, name="offsets")
-        w_raw = keep.tile([P, PACK, M], F32, name="w_raw", align_bytes=64)
-        w_bf = keep.tile([P, M, PACK], BF16, name="w_bf", align_bytes=64)
-        w_codes = keep.tile([P, M], U32, name="w_codes", align_bytes=64)
-        w_scales = keep.tile([P, M], U8, name="w_scales", align_bytes=64)
+        w_raw = [keep.tile([P, PACK, P], F32, name=f"w_raw{m}", align_bytes=64) for m in range(BLOCKS)]
+        w_bf = [keep.tile([P, P, PACK], BF16, name=f"w_bf{m}", align_bytes=64) for m in range(BLOCKS)]
+        w_codes = [keep.tile([P, P], U32, name=f"w_codes{m}", align_bytes=64) for m in range(BLOCKS)]
+        w_scales = [keep.tile([P, P], U8, name=f"w_scales{m}", align_bytes=64) for m in range(BLOCKS)]
         x_codes = keep.tile([P, S], U32, name="x_codes", align_bytes=64)
         x_scales = keep.tile([P, S], U8, name="x_scales", align_bytes=64)
-        x_raw = [keep.tile([P, PACK, n], F32, name=f"x_raw{c}", align_bytes=64) for c, (s0, n) in enumerate(CHUNKS)]
-        x_bf = [keep.tile([P, n, PACK], BF16, name=f"x_bf{c}", align_bytes=64) for c, (s0, n) in enumerate(CHUNKS)]
+        x_raw = [keep.tile([P, PACK, n], F32, name=f"x_raw{c}", align_bytes=64) for c, (s0, n) in enumerate(X_CHUNKS)]
+        x_bf = [keep.tile([P, n, PACK], BF16, name=f"x_bf{c}", align_bytes=64) for c, (s0, n) in enumerate(X_CHUNKS)]
         bias = [keep.tile([P, 1], F32, name=f"bias{m}") for m in range(BLOCKS)]
         gates = [keep.tile([P, S], F32, name=f"gate{m}", align_bytes=64) for m in range(BLOCKS)]
+        y = [keep.tile([P, S], F32, name=f"y{m}", align_bytes=64) for m in range(BLOCKS)]
         window = [keep.tile([P, T], F32, name=f"window{m}", align_bytes=64) for m in range(BLOCKS)]
         warm = keep.tile([P, 1], F32, name="warm")
         warm_out = keep.tile([P, 1], F32, name="warm_out")
 
+        def load_w(m):
+            nc.sync.dma_start(w_raw[m][:], w[:, m * P : (m + 1) * P].rearrange("(p j) m -> p j m", j=PACK))
+
         def load_x(c):
-            s0, n = CHUNKS[c]
+            s0, n = X_CHUNKS[c]
             nc.sync.dma_start(x_raw[c][:], xT[:, s0 : s0 + n].rearrange("(p j) n -> p j n", j=PACK))
 
-        nc.sync.dma_start(w_raw[:], w.rearrange("(p j) m -> p j m", j=PACK))
-        load_x(0)
-        nc.sync.dma_start(offsets[:], offs)
-        load_x(1)
-        nc.sync.dma_start(gates[0][:], gate[0:P, :])
-        nc.sync.dma_start(gates[1][:], gate[P : 2 * P, :])
-        load_x(2)
-        load_x(3)
-        for m in range(BLOCKS):
-            nc.scalar.dma_start(bias[m][:], b[m * P : (m + 1) * P, :])
-
-        nc.vector.memset(warm[:], 0.0)
-        nc.scalar.activation(warm_out[:], warm[:], SILU)
-        for m in range(BLOCKS):
-            nc.vector.memset(window[m][:], 0.0)
+        def load_gate(m, lo, hi):
+            nc.sync.dma_start(gates[m][:, lo:hi], gate[m * P : (m + 1) * P, lo:hi])
 
         def interleave(copy, dst, src, lo, hi):
             copy(dst[:, lo:hi, :], src[:, :, lo:hi].rearrange("p j n -> p n j"))
 
-        def quantize(dst, scales, src, lo, hi):
+        def convert(dst, src, n, vector_columns):
+            if vector_columns > 0:
+                interleave(nc.vector.tensor_copy, dst, src, 0, vector_columns)
+            if vector_columns < n:
+                interleave(nc.scalar.copy, dst, src, vector_columns, n)
+
+        def quantize(codes, scales, src, lo, hi):
             nc.vector.quantize_mx(
-                out=dst[:, lo:hi].bitcast(FP8X4),
+                out=codes[:, lo:hi].bitcast(FP8X4),
                 scales=scales[:, lo:hi],
                 in_=src[:].rearrange("p n j -> p (n j)"),
             )
 
-        interleave(nc.scalar.copy, w_bf, w_raw, 0, P)
-        interleave(nc.vector.tensor_copy, w_bf, w_raw, P, M)
-        quantize(w_codes, w_scales, w_bf, 0, M)
-        def prepare(c):
-            s0, n = CHUNKS[c]
-            interleave(nc.vector.tensor_copy if c < 2 else nc.scalar.copy, x_bf[c], x_raw[c], 0, n)
+        def quantize_w(m, vector_columns):
+            convert(w_bf[m], w_raw[m], P, vector_columns)
+            quantize(w_codes[m], w_scales[m], w_bf[m], 0, P)
+
+        def quantize_x(c, vector_columns):
+            s0, n = X_CHUNKS[c]
+            convert(x_bf[c], x_raw[c], n, vector_columns)
             quantize(x_codes, x_scales, x_bf[c], s0, s0 + n)
 
-        prepare(0)
-        pending = []
-        for c, (s0, n) in enumerate(CHUNKS):
-            ys = []
-            for m in range(BLOCKS):
-                acc = psum.tile([P, n], F32, name=f"acc{c}_{m}")
-                nc.tensor.matmul_mx(
-                    out=acc[:],
-                    lhsT=w_codes[:, m * P : (m + 1) * P].bitcast(FP8X4),
-                    lhsT_scale=w_scales[:, m * P : (m + 1) * P],
-                    rhs=x_codes[:, s0 : s0 + n].bitcast(FP8X4),
-                    rhs_scale=x_scales[:, s0 : s0 + n],
-                    start=True,
-                    stop=True,
-                )
-                y = keep.tile([P, n], F32, name=f"y{c}_{m}", align_bytes=64)
-                nc.scalar.activation(y[:], acc[:], SILU, bias=bias[m][:])
-                ys.append(y)
-            if c + 1 < len(CHUNKS):
-                prepare(c + 1)
-            pending.append((s0, n, ys))
-            if c != len(CHUNKS) - 2:
-                for m in range(BLOCKS):
-                    for p0, pn, pys in pending:
-                        nc.vector.tensor_tensor(
-                            window[m][:].indirect(offsets[:, p0 // 16 : (p0 + pn) // 16]),
-                            pys[m][:],
-                            gates[m][:, p0 : p0 + pn],
-                            MULT,
-                        )
-                    if c == len(CHUNKS) - 1:
-                        nc.sync.dma_start(out[m * P : (m + 1) * P, :], window[m][:])
-                pending = []
+        def layer(m, lo, hi):
+            acc = psum.tile([P, hi - lo], F32, name=f"acc{m}_{lo}")
+            nc.tensor.matmul_mx(
+                out=acc[:],
+                lhsT=w_codes[m][:].bitcast(FP8X4),
+                lhsT_scale=w_scales[m][:],
+                rhs=x_codes[:, lo:hi].bitcast(FP8X4),
+                rhs_scale=x_scales[:, lo:hi],
+                start=True,
+                stop=True,
+            )
+            nc.scalar.activation(y[m][:, lo:hi], acc[:], SILU, bias=bias[m][:])
+
+        def place(m, lo, hi):
+            nc.vector.tensor_tensor(
+                window[m][:].indirect(offsets[:, lo // 16 : hi // 16]),
+                y[m][:, lo:hi],
+                gates[m][:, lo:hi],
+                MULT,
+            )
+
+        def store(m):
+            nc.sync.dma_start(out[m * P : (m + 1) * P, :], window[m][:])
+
+        load_w(0)
+        load_x(0)
+        nc.scalar.dma_start(bias[0][:], b[0:P, :])
+        nc.scalar.dma_start(bias[1][:], b[P : 2 * P, :])
+        nc.sync.dma_start(offsets[:], offs)
+        load_x(1)
+        load_gate(0, 0, S)
+        load_x(2)
+        load_w(1)
+        load_x(3)
+        load_gate(1, 0, S)
+        nc.vector.memset(warm[:], 0.0)
+        nc.scalar.activation(warm_out[:], warm[:], SILU)
+        nc.vector.memset(window[0][:], 0.0)
+        nc.vector.memset(window[1][:], 0.0)
+        quantize_w(0, 80)
+        quantize_x(0, 80)
+        layer(0, 0, 128)
+        quantize_x(1, 128)
+        layer(0, 128, 256)
+        place(0, 0, 128)
+        quantize_x(2, 64)
+        layer(0, 256, 384)
+        quantize_w(1, 0)
+        layer(1, 0, 256)
+        place(0, 128, 256)
+        place(0, 256, 384)
+        quantize_x(3, 0)
+        layer(0, 384, 512)
+        layer(1, 256, 512)
+        place(1, 0, 256)
+        place(0, 384, 512)
+        store(0)
+        place(1, 256, 512)
+        store(1)

@@ -53,7 +53,10 @@ def tile_picked_place_lin_silu_sub_l_kernel(tc, xT, w, b, gate, offs, out):
             nc.sync.dma_start(gates[m][:, lo:hi], gate[m * P : (m + 1) * P, lo:hi])
 
         def interleave(copy, dst, src, lo, hi):
-            copy(dst[:, lo:hi, :], src[:, :, lo:hi].rearrange("p j n -> p n j"))
+            copy(
+                dst[:, lo:hi, :].rearrange("p (c i) j -> p c j i", i=4),
+                src[:, :, lo:hi].rearrange("p j (c i) -> p c j i", i=4),
+            )
 
         def convert(dst, src, n, vector_columns):
             if vector_columns > 0:

from contextlib import ExitStack

import concourse.mybir as mybir

K, T, S, M = 512, 1024, 512, 256
FLOPS = 2 * K * S * M

F32 = mybir.dt.float32
BF16 = mybir.dt.bfloat16
U32 = mybir.dt.uint32
U16 = mybir.dt.uint16
U8 = mybir.dt.uint8
FP8X4 = mybir.dt.float8_e4m3fn_x4
SILU = mybir.ActivationFunctionType.Silu
MULT = mybir.AluOpType.mult

P = 128
PACK = 4
BLOCKS = M // P
X_CHUNKS = ((0, 128), (128, 128), (256, 128), (384, 128))


def tile_picked_place_lin_silu_sub_l_kernel(tc, xT, w, b, gate, offs, out):
    nc = tc.nc
    with ExitStack() as ctx:
        keep = ctx.enter_context(tc.tile_pool(name="keep", bufs=1))
        psum = ctx.enter_context(tc.psum_pool(name="psum", bufs=1))

        offsets = keep.tile([P, S // 16], U16, name="offsets")
        w_raw = [keep.tile([P, PACK, P], F32, name=f"w_raw{m}", align_bytes=64) for m in range(BLOCKS)]
        w_bf = [keep.tile([P, P, PACK], BF16, name=f"w_bf{m}", align_bytes=64) for m in range(BLOCKS)]
        w_codes = [keep.tile([P, P], U32, name=f"w_codes{m}", align_bytes=64) for m in range(BLOCKS)]
        w_scales = [keep.tile([P, P], U8, name=f"w_scales{m}", align_bytes=64) for m in range(BLOCKS)]
        x_codes = keep.tile([P, S], U32, name="x_codes", align_bytes=64)
        x_scales = keep.tile([P, S], U8, name="x_scales", align_bytes=64)
        x_raw = [keep.tile([P, PACK, n], F32, name=f"x_raw{c}", align_bytes=64) for c, (s0, n) in enumerate(X_CHUNKS)]
        x_bf = [keep.tile([P, n, PACK], BF16, name=f"x_bf{c}", align_bytes=64) for c, (s0, n) in enumerate(X_CHUNKS)]
        bias = [keep.tile([P, 1], F32, name=f"bias{m}") for m in range(BLOCKS)]
        gates = [keep.tile([P, S], F32, name=f"gate{m}", align_bytes=64) for m in range(BLOCKS)]
        y = [keep.tile([P, S], F32, name=f"y{m}", align_bytes=64) for m in range(BLOCKS)]
        window = [keep.tile([P, T], F32, name=f"window{m}", align_bytes=64) for m in range(BLOCKS)]
        warm = keep.tile([P, 1], F32, name="warm")
        warm_out = keep.tile([P, 1], F32, name="warm_out")

        def load_w(m):
            nc.sync.dma_start(w_raw[m][:], w[:, m * P : (m + 1) * P].rearrange("(p j) m -> p j m", j=PACK))

        def load_x(c):
            s0, n = X_CHUNKS[c]
            nc.sync.dma_start(x_raw[c][:], xT[:, s0 : s0 + n].rearrange("(p j) n -> p j n", j=PACK))

        def load_gate(m, lo, hi):
            nc.sync.dma_start(gates[m][:, lo:hi], gate[m * P : (m + 1) * P, lo:hi])

        def interleave(copy, dst, src, lo, hi):
            copy(
                dst[:, lo:hi, :].rearrange("p (c i) j -> p c j i", i=4),
                src[:, :, lo:hi].rearrange("p j (c i) -> p c j i", i=4),
            )

        def convert(dst, src, n, vector_columns):
            if vector_columns > 0:
                interleave(nc.vector.tensor_copy, dst, src, 0, vector_columns)
            if vector_columns < n:
                interleave(nc.scalar.copy, dst, src, vector_columns, n)

        def quantize(codes, scales, src, lo, hi):
            nc.vector.quantize_mx(
                out=codes[:, lo:hi].bitcast(FP8X4),
                scales=scales[:, lo:hi],
                in_=src[:].rearrange("p n j -> p (n j)"),
            )

        def quantize_w(m, vector_columns):
            convert(w_bf[m], w_raw[m], P, vector_columns)
            quantize(w_codes[m], w_scales[m], w_bf[m], 0, P)

        def quantize_x(c, vector_columns):
            s0, n = X_CHUNKS[c]
            convert(x_bf[c], x_raw[c], n, vector_columns)
            quantize(x_codes, x_scales, x_bf[c], s0, s0 + n)

        def layer(m, lo, hi):
            acc = psum.tile([P, hi - lo], F32, name=f"acc{m}_{lo}")
            nc.tensor.matmul_mx(
                out=acc[:],
                lhsT=w_codes[m][:].bitcast(FP8X4),
                lhsT_scale=w_scales[m][:],
                rhs=x_codes[:, lo:hi].bitcast(FP8X4),
                rhs_scale=x_scales[:, lo:hi],
                start=True,
                stop=True,
            )
            nc.scalar.activation(y[m][:, lo:hi], acc[:], SILU, bias=bias[m][:])

        def place(m, lo, hi):
            nc.vector.tensor_tensor(
                window[m][:].indirect(offsets[:, lo // 16 : hi // 16]),
                y[m][:, lo:hi],
                gates[m][:, lo:hi],
                MULT,
            )

        def store(m):
            nc.sync.dma_start(out[m * P : (m + 1) * P, :], window[m][:])

        load_w(0)
        load_x(0)
        nc.scalar.dma_start(bias[0][:], b[0:P, :])
        nc.scalar.dma_start(bias[1][:], b[P : 2 * P, :])
        nc.sync.dma_start(offsets[:], offs)
        load_x(1)
        load_gate(0, 0, S)
        load_x(2)
        load_w(1)
        load_x(3)
        load_gate(1, 0, S)
        nc.vector.memset(warm[:], 0.0)
        nc.scalar.activation(warm_out[:], warm[:], SILU)
        nc.vector.memset(window[0][:], 0.0)
        nc.vector.memset(window[1][:], 0.0)
        quantize_w(0, 80)
        quantize_x(0, 80)
        layer(0, 0, 128)
        quantize_x(1, 128)
        layer(0, 128, 256)
        place(0, 0, 128)
        quantize_x(2, 64)
        layer(0, 256, 384)
        quantize_w(1, 0)
        layer(1, 0, 256)
        place(0, 128, 256)
        place(0, 256, 384)
        quantize_x(3, 0)
        layer(0, 384, 512)
        layer(1, 256, 512)
        place(1, 0, 256)
        place(0, 384, 512)
        store(0)
        place(1, 256, 512)
        store(1)
